import numpy as np
import ml_dtypes


def mxq(x, axis, fmt="e4m3"):
    dtype, down = {"e4m3": (ml_dtypes.float8_e4m3fn, 7), "e5m2": (ml_dtypes.float8_e5m2, 14)}[fmt]
    v = np.moveaxis(np.asarray(x, np.float32).astype(ml_dtypes.bfloat16).astype(np.float64), axis, -1)
    blocks = v.reshape(v.shape[:-1] + (-1, 32))
    amax = np.abs(blocks).max(-1, keepdims=True)
    byte = np.maximum(np.where(amax > 0, np.frexp(amax)[1] - 1 + 127, 0) - down, 1)
    scale = np.exp2(byte - 127.0)
    codes = (blocks / scale).astype(np.float32).astype(dtype).astype(np.float64)
    return np.moveaxis((codes * scale).reshape(v.shape), -1, axis)


WIDE = False


def mx_kscale(k):
    if not WIDE:
        return np.ones(k)
    levels = np.array([10, -10, 5, -5, 0])
    if k % 512:
        return np.exp2(np.random.permutation(np.resize(levels, k // 32))).repeat(32)
    a = np.empty((k // 512, 16))
    for p in range(k // 512):
        a[p, :8] = np.random.permutation(np.resize(levels, 8))
        for g in range(8):
            far = levels[np.abs(levels - a[p, g]) >= 10]
            a[p, g + 8] = far[np.random.randint(len(far))]
    return np.exp2(a.ravel()).repeat(32)


def f64(x):
    return np.asarray(x).astype(np.float64)


def striped(idx):
    return np.tile(idx.reshape(-1, 16).T, (8, 1)).astype(np.uint16)


def unstriped(offs):
    return offs[:16].T.reshape(-1).astype(np.int64)


E2M1 = np.array([0.0, 0.5, 1.0, 1.5, 2.0, 3.0, 4.0, 6.0, -0.0, -0.5, -1.0, -1.5, -2.0, -3.0, -4.0, -6.0])


def pack_weight(w, fmt):
    k, n = w.shape
    w = f64(np.asarray(w, np.float32).astype(ml_dtypes.bfloat16)).reshape(k // 32, 32, n)
    amax = np.abs(w).max(1)
    if fmt == "e4m3":
        byte = np.frexp(amax)[1] - 1 + 127 - 7
    else:
        mant, ex = np.frexp(amax / 6.0)
        byte = np.where(mant > 0.5, ex, ex - 1) + 127
    byte = np.clip(np.where(amax > 0, byte, 1), 1, 254)
    scaled = (w * np.exp2(127.0 - byte)[:, None, :]).reshape(k, n).astype(np.float32)
    by_word = np.ascontiguousarray(scaled.reshape(k // 512, 128, 4, n).transpose(0, 1, 3, 2))
    if fmt == "e4m3":
        words = by_word.astype(ml_dtypes.float8_e4m3fn).view(np.uint8)
    else:
        c = by_word.astype(ml_dtypes.float4_e2m1fn).view(np.uint8) & 0xF
        words = (c[..., 0::2] | (c[..., 1::2] << 4)).reshape(k // 512, 128, 2 * n)
    return np.ascontiguousarray(words), np.ascontiguousarray(byte.astype(np.uint8).reshape(k // 512, 16, n))


def unpack_weight(words, scales, fmt):
    g, _, n = scales.shape
    words = np.ascontiguousarray(words).reshape(g, 128, n, -1)
    if fmt == "e4m3":
        vals = words.view(ml_dtypes.float8_e4m3fn).astype(np.float64)
    else:
        nib = np.empty((g, 128, n, 4), np.uint8)
        nib[..., 0::2] = words & 0xF
        nib[..., 1::2] = words >> 4
        vals = E2M1[nib]
    vals = vals * np.repeat(np.exp2(scales.astype(np.float64) - 127.0), 8, axis=1)[..., None]
    return vals.transpose(0, 1, 3, 2).reshape(g * 512, n)


def gelu(v):
    return 0.5 * v * (1.0 + np.tanh(np.sqrt(2.0 / np.pi) * (v + 0.044715 * v**3)))


K, K2, H, N, T, S, T2, P = 1024, 512, 1024, 512, 4096, 1024, 2048, 512

def setup_inputs():
    n = np.random.standard_normal
    s, s2, u = mx_kscale(K)[:, None], mx_kscale(K2)[:, None], mx_kscale(H)[:, None]
    tab_words, tab_scales = pack_weight(n((K, T)) * s, "e4m3")
    w2_words, w2_scales = pack_weight(0.8 * n((K2, H)) / np.sqrt(K2) / s2, "e2m1")
    perm = np.random.permutation(T2)
    return {
        "tab_words": tab_words, "tab_scales": tab_scales,
        "offs": striped(np.random.permutation(T)[:S]),
        "offs2": striped(np.random.permutation(T2)[:S]),
        "offs3": striped(perm[:P]),
        "offs4": striped(perm[P:2 * P]),
        "w1": (n((K, H)) / np.sqrt(K) / s).astype(np.float32),
        "side": (n((K2, S)) * s2).astype(np.float32),
        "w2_words": w2_words, "w2_scales": w2_scales,
        "gain": (1.4 * np.exp(0.4 * n(H)) * u[:, 0]).astype(np.float32),
        "wgs": np.exp(0.3 * n((128, S))).astype(np.float32),
        "page0": (n((H, T2)) * u).astype(np.float32),
        "shift": (0.7 * n(H) * u[:, 0]).astype(np.float32),
        "w3": (n((H, N)) / np.sqrt(H) / u).astype(np.float32),
        "marks": np.exp(0.4 * n((N, T2))).astype(np.float32),
    }

def reference(tab_words, tab_scales, offs, offs2, offs3, offs4, w1, side, w2_words, w2_scales, gain, wgs, page0, shift, w3, marks):
    v = unpack_weight(tab_words, tab_scales, "e4m3")[:, unstriped(offs)]
    w2 = unpack_weight(w2_words, w2_scales, "e2m1")
    w1q = mxq(f64(w1), 0, "e4m3")
    sq = mxq(f64(side), 0, "e4m3")
    z = w1q.T @ v + w2.T @ sq
    h = f64(gain)[:, None] * (0.5 * z * (1.0 + np.tanh(np.sqrt(2.0 / np.pi) * (z + 0.044715 * z ** 3))))
    page = f64(page0).copy()
    page[:, unstriped(offs2)] = np.tile(f64(wgs), (H // 128, 1)) * h
    a = page[:, unstriped(offs3)]
    b = page[:, unstriped(offs4)]
    page[:, unstriped(offs3)] = np.minimum(a, b)
    page[:, unstriped(offs4)] = a + b
    xq = mxq(page + f64(shift)[:, None], 0, "e4m3")
    w3q = mxq(f64(w3), 0, "e4m3")
    return (w3q.T @ xq) * f64(marks)

@@ -1,0 +1,302 @@
+from contextlib import ExitStack
+
+import concourse.mybir as mybir
+
+K, K2, H, N, T, S, T2, PAIRS = 1024, 512, 1024, 512, 4096, 1024, 2048, 512
+FLOPS = 2 * (K * H * S + K2 * H * S + H * N * T2)
+
+F32 = mybir.dt.float32
+BF16 = mybir.dt.bfloat16
+I32 = mybir.dt.int32
+U32 = mybir.dt.uint32
+U16 = mybir.dt.uint16
+U8 = mybir.dt.uint8
+E4M3 = mybir.dt.float8_e4m3fn_x4
+E2M1 = mybir.dt.float4_e2m1fn_x4
+ACT = mybir.ActivationFunctionType
+ALU = mybir.AluOpType
+
+P = 128
+PACK = 4
+PASS = P * PACK
+COLS = 512
+ROW_TILES = H // P
+CHUNKS = T2 // COLS
+N_TILES = N // P
+BANKS = 8
+PAGE_BYTES = T2 * 4
+SLOT_BYTES = PACK * COLS * 2
+
+
+def tile_list_stumpage_stand_appraisal_kernel(
+    tc, tab_words, tab_scales, offs, offs2, offs3, offs4, w1, side, w2_words, w2_scales,
+    gain, wgs, page0, shift, w3, marks, out,
+):
+    nc = tc.nc
+    with ExitStack() as ctx:
+        lists = ctx.enter_context(tc.tile_pool(name="lists", bufs=1))
+        keep = ctx.enter_context(tc.tile_pool(name="keep", bufs=1))
+        big = ctx.enter_context(tc.tile_pool(name="big", bufs=1))
+        slots = ctx.enter_context(tc.tile_pool(name="slots", bufs=1))
+        ring = ctx.enter_context(tc.tile_pool(name="ring", bufs=2))
+        psum = ctx.enter_context(tc.psum_pool(name="psum", bufs=1))
+
+        banks = [psum.tile([P, COLS], F32, name="bank%d" % b) for b in range(BANKS)]
+
+        def load_list(src, name):
+            tile = lists.tile(list(src.shape), U16, name=name)
+            nc.sync.dma_start(tile[:], src)
+            return tile
+
+        def mx_tiles(name):
+            codes = keep.tile([P, COLS], U32, name=name + "_codes", align_bytes=64)
+            scales = keep.tile([P, COLS], U8, name=name + "_scales", align_bytes=64)
+            return codes, scales
+
+        def load_rows(rows):
+            raw = ring.tile([P, PACK, COLS], F32, name="raw", bufs=3)
+            nc.sync.dma_start(raw[:], rows.rearrange("(p j) c -> p j c", j=PACK))
+            return raw
+
+        def quantize(woven, name):
+            codes, scales = mx_tiles(name)
+            nc.vector.quantize_mx(codes[:].bitcast(E4M3), scales[:], woven[:])
+            return codes, scales
+
+        def slot_tile(shape, dtype, name, slot):
+            return slots.tile(shape, dtype, name=name, offset=slot * SLOT_BYTES, align_bytes=64)
+
+        def quantize_rows(raw, name, slot):
+            woven = slot_tile([P, PACK * COLS], BF16, name + "_woven", slot)
+            nc.scalar.copy(
+                woven[:].rearrange("p (c i j) -> p c j i", i=4, j=PACK),
+                raw[:].rearrange("p j (c i) -> p c j i", i=4),
+            )
+            return quantize(woven, name)
+
+        def quantize_rows_dealt(raw, name, slot):
+            woven = slot_tile([P, PACK * COLS], BF16, name + "_woven", slot)
+            nc.scalar.copy(
+                woven[:].rearrange("p (t m j) -> p m t j", t=PACK, j=PACK),
+                raw[:].rearrange("p j (m t) -> p m t j", t=PACK),
+            )
+            return quantize(woven, name)
+
+        page_rows = page0.rearrange("(b p t) c -> b t p c", b=H // PASS, t=PACK)
+
+        def load_page(i):
+            page = big.tile([P, T2], F32, name="page%d" % i, offset=i * PAGE_BYTES)
+            nc.sync.dma_start(page[:], page_rows[i // PACK, i % PACK])
+            return page
+
+        wgs_rows = wgs.rearrange("(q t) j -> t q j", t=PACK)
+
+        def load_wgs(t, cols, name):
+            tile = keep.tile([P, cols.stop - cols.start], F32, name=name)
+            for quad in range(4):
+                nc.sync.dma_start(tile[32 * quad : 32 * quad + 32, :], wgs_rows[t][:, cols])
+            return tile
+
+        halves = [slice(0, COLS), slice(COLS, 2 * COLS)]
+
+        tab_planes = slot_tile([P, T], U8, "tab_planes", 4)
+        nc.vector.memset(tab_planes[:].bitcast(I32), 0)
+        w2_plane_raw = slot_tile([P, H], U8, "w2_plane_raw", 5)
+        nc.vector.memset(w2_plane_raw[:].bitcast(I32), 0)
+
+        w1_raw = [load_rows(w1[a * PASS : (a + 1) * PASS, halves[0]]) for a in range(2)]
+        idx = load_list(offs, "idx")
+        w2_raw = slot_tile([P, 2 * H], U8, "w2_raw", 6)
+        nc.sync.dma_start(w2_raw[:].bitcast(I32), w2_words[0].bitcast(I32))
+        for quad in range(4):
+            nc.sync.dma_start(
+                tab_planes[32 * quad : 32 * quad + 8, :].bitcast(I32),
+                tab_scales[:, 4 * quad : 4 * quad + 4, :].bitcast(I32),
+            )
+        side_raw = load_rows(side[:, halves[0]])
+        for quad in range(4):
+            nc.sync.dma_start(
+                w2_plane_raw[32 * quad : 32 * quad + 4, :].bitcast(I32),
+                w2_scales[0, 4 * quad : 4 * quad + 4, :].bitcast(I32),
+            )
+        tab = []
+        for a in range(2):
+            words = big.tile([P, T], U32, name="tab%d" % a, offset=(4 + 2 * a) * PAGE_BYTES)
+            nc.sync.dma_start(words[:].bitcast(I32), tab_words[a].rearrange("p t i -> p (t i)").bitcast(I32))
+            tab.append(words)
+        gain_sb = keep.tile([P, H // PASS, PACK], F32, name="gain_sb")
+        nc.sync.dma_start(gain_sb[:], gain.rearrange("(b p t) -> p b t", b=H // PASS, t=PACK))
+        idx2 = load_list(offs2, "idx2")
+        wg = {(0, 0): load_wgs(0, halves[0], "wg0_0")}
+        pages = [load_page(0)]
+
+        w1_q = {(0, 0): quantize_rows_dealt(w1_raw[0], "w1_00", 0)}
+        picked_planes = keep.tile([P, S], U8, name="picked_planes", align_bytes=64)
+        nc.vector.tensor_copy(picked_planes[:], tab_planes[:].indirect(idx[:]))
+        w2_codes = keep.tile([P, 2 * H], U8, name="w2_codes", align_bytes=64)
+        nc.vector.tensor_copy(
+            w2_codes[:].rearrange("p (b t m e) -> p b t m e", b=2, t=PACK, e=2),
+            w2_raw[:].rearrange("p (b m t e) -> p b t m e", b=2, t=PACK, e=2),
+        )
+        w1_q[1, 0] = quantize_rows_dealt(w1_raw[1], "w1_10", 1)
+        side_q = [quantize_rows(side_raw, "side0", 2)]
+        w2_plane = keep.tile([P, H], U8, name="w2_plane", align_bytes=64)
+        nc.vector.tensor_copy(
+            w2_plane[:].rearrange("p (b t m) -> p b t m", b=2, t=PACK),
+            w2_plane_raw[:].rearrange("p (b m t) -> p b t m", b=2, t=PACK),
+        )
+
+        picked = {}
+
+        def pick_words(a, half):
+            tile = keep.tile([P, COLS], U32, name="picked%d_%d" % (a, half), align_bytes=64)
+            nc.vector.tensor_copy(tile[:], tab[a][:].indirect(idx[:, 32 * half : 32 * half + 32]))
+            picked[a, half] = tile
+
+        h = {}
+
+        def first_stage(i, half):
+            b, t = divmod(i, PACK)
+            bank = banks[half]
+            nc.tensor.matmul_mx(
+                bank[:],
+                lhsT=w2_codes[:, 2 * P * i : 2 * P * (i + 1)].bitcast(E2M1),
+                lhsT_scale=w2_plane[:, P * i : P * (i + 1)],
+                rhs=side_q[half][0][:].bitcast(E4M3),
+                rhs_scale=side_q[half][1][:],
+                start=True,
+                stop=False,
+            )
+            for a in range(2):
+                codes, scales = w1_q[a, b]
+                nc.tensor.matmul_mx(
+                    bank[:],
+                    lhsT=codes[:, P * t : P * (t + 1)].bitcast(E4M3),
+                    lhsT_scale=scales[:, P * t : P * (t + 1)],
+                    rhs=picked[a, half][:].bitcast(E4M3),
+                    rhs_scale=picked_planes[4 * a :, halves[half]],
+                    start=False,
+                    stop=(a == 1),
+                )
+            tile = ring.tile([P, COLS], F32, name="h", tag="slab", bufs=16)
+            nc.scalar.activation(tile[:], bank[:], ACT.Gelu_apprx_tanh)
+            nc.scalar.activation(tile[:], tile[:], ACT.Copy, scale=gain_sb[:, b, t : t + 1])
+            h[i, half] = tile
+
+        def put_h(i, half):
+            nc.vector.tensor_tensor(
+                pages[i][:].indirect(idx2[:, 32 * half : 32 * half + 32]),
+                h[i, half][:],
+                wg[i % PACK, half][:],
+                ALU.mult,
+            )
+
+        pick_words(0, 0)
+        pick_words(0, 1)
+        pick_words(1, 0)
+        first_stage(0, 0)
+        pick_words(1, 1)
+        put_h(0, 0)
+
+        side_raw = load_rows(side[:, halves[1]])
+        wg[0, 1] = load_wgs(0, halves[1], "wg0_1")
+        idx3 = load_list(offs3, "idx3")
+        idx4 = load_list(offs4, "idx4")
+        side_q.append(quantize_rows(side_raw, "side1", 3))
+        first_stage(0, 1)
+        put_h(0, 1)
+
+        def prepare(i):
+            if i < PACK:
+                both = load_wgs(i, slice(0, S), "wg%d" % i)
+                wg[i, 0], wg[i, 1] = both[:, halves[0]], both[:, halves[1]]
+            pages.append(load_page(i))
+            first_stage(i, 0)
+            first_stage(i, 1)
+
+        prepare(1)
+        shift_sb = keep.tile([P, H // PASS, PACK], F32, name="shift_sb")
+        nc.sync.dma_start(shift_sb[:], shift.rearrange("(b p t) -> p b t", b=H // PASS, t=PACK))
+        for a in range(2):
+            w1_q[a, 1] = quantize_rows_dealt(load_rows(w1[a * PASS : (a + 1) * PASS, halves[1]]), "w1_%d1" % a, a)
+        prepare(2)
+        w3_q = [quantize_rows(load_rows(w3[b * PASS : (b + 1) * PASS, :]), "w3_%d" % b, 6 + b) for b in range(2)]
+        for i in range(3, ROW_TILES):
+            prepare(i)
+
+        woven_page = {
+            (b, c): slot_tile([P, COLS, PACK], BF16, "woven_page%d%d" % (b, c), CHUNKS * b + c)
+            for b in range(H // PASS)
+            for c in range(CHUNKS)
+        }
+        page_q = {}
+
+        def quantize_page(b, c):
+            codes, scales = mx_tiles("page_%d%d" % (b, c))
+            nc.vector.quantize_mx(codes[:].bitcast(E4M3), scales[:], woven_page[b, c][:].rearrange("p c t -> p (c t)"))
+            page_q[b, c] = codes, scales
+
+        def bank_of(c, n):
+            return banks[(c * N_TILES + n + 2) % BANKS]
+
+        def second_stage(b, c, n):
+            nc.tensor.matmul_mx(
+                bank_of(c, n)[:],
+                lhsT=w3_q[b][0][:, P * n : P * (n + 1)].bitcast(E4M3),
+                lhsT_scale=w3_q[b][1][:, P * n : P * (n + 1)],
+                rhs=page_q[b, c][0][:].bitcast(E4M3),
+                rhs_scale=page_q[b, c][1][:],
+                start=(b == 0),
+                stop=(b == 1),
+            )
+
+        marks_sb = []
+        for i in range(ROW_TILES):
+            b, t = divmod(i, PACK)
+            page = pages[i]
+            if i + 1 < ROW_TILES:
+                first = ring.tile([P, PAIRS], F32, name="first")
+            else:
+                first = slot_tile([P, PAIRS], F32, "first_last", CHUNKS - 1)
+            second = ring.tile([P, PAIRS], F32, name="second")
+            lower = ring.tile([P, PAIRS], F32, name="lower")
+            nc.vector.tensor_copy(first[:], page[:].indirect(idx3[:]))
+            nc.vector.tensor_copy(second[:], page[:].indirect(idx4[:]))
+            if i + 1 < ROW_TILES:
+                put_h(i + 1, 0)
+            nc.vector.tensor_tensor(lower[:], first[:], second[:], ALU.min)
+            nc.vector.tensor_tensor(page[:].indirect(idx4[:]), first[:], second[:], ALU.add)
+            if i + 1 < ROW_TILES:
+                put_h(i + 1, 1)
+            if i == PACK:
+                for c in range(CHUNKS):
+                    quantize_page(0, c)
+                for c in range(BANKS // N_TILES):
+                    for n in range(N_TILES):
+                        second_stage(0, c, n)
+            nc.vector.tensor_copy(page[:].indirect(idx3[:]), lower[:])
+            for c in range(CHUNKS):
+                nc.scalar.activation(
+                    woven_page[b, c][:, :, t],
+                    page[:, c * COLS : (c + 1) * COLS],
+                    ACT.Identity,
+                    bias=shift_sb[:, b, t : t + 1],
+                )
+            if i < N_TILES:
+                tile = big.tile([P, T2], F32, name="marks%d" % i, offset=i * PAGE_BYTES)
+                nc.sync.dma_start(tile[:], marks[P * i : P * (i + 1), :])
+                marks_sb.append(tile)
+
+        quantize_page(1, 0)
+        for c in range(CHUNKS):
+            for n in range(N_TILES):
+                if c >= BANKS // N_TILES:
+                    second_stage(0, c, n)
+                second_stage(1, c, n)
+            if c + 1 < CHUNKS:
+                quantize_page(1, c + 1)
+            for n in range(N_TILES):
+                cols = slice(c * COLS, (c + 1) * COLS)
+                result = ring.tile([P, COLS], F32, name="result", tag="slab", bufs=16)
+                nc.vector.tensor_tensor(result[:], bank_of(c, n)[:], marks_sb[n][:, cols], ALU.mult)
+                nc.sync.dma_start(out[P * n : P * (n + 1), cols], result[:])

@@ -20,6 +20,7 @@ P = 128
 PACK = 4
 PASS = P * PACK
 COLS = 512
+QUARTER = 256
 ROW_TILES = H // P
 CHUNKS = T2 // COLS
 N_TILES = N // P
@@ -91,11 +92,11 @@ def tile_list_stumpage_stand_appraisal_kernel(
 
         wgs_rows = wgs.rearrange("(q t) j -> t q j", t=PACK)
 
-        def load_wgs(t, cols, name):
-            tile = keep.tile([P, cols.stop - cols.start], F32, name=name)
+        wg = [keep.tile([P, S], F32, name="wg%d" % t) for t in range(PACK)]
+
+        def load_wgs(t, cols):
             for quad in range(4):
-                nc.sync.dma_start(tile[32 * quad : 32 * quad + 32, :], wgs_rows[t][:, cols])
-            return tile
+                nc.sync.dma_start(wg[t][32 * quad : 32 * quad + 32, cols], wgs_rows[t][:, cols])
 
         halves = [slice(0, COLS), slice(COLS, 2 * COLS)]
 
@@ -104,124 +105,131 @@ def tile_list_stumpage_stand_appraisal_kernel(
         w2_plane_raw = slot_tile([P, H], U8, "w2_plane_raw", 5)
         nc.vector.memset(w2_plane_raw[:].bitcast(I32), 0)
 
+        def load_tab(a):
+            words = big.tile([P, T], U32, name="tab%d" % a, offset=(4 + 2 * a) * PAGE_BYTES)
+            nc.sync.dma_start(words[:].bitcast(I32), tab_words[a].rearrange("p t i -> p (t i)").bitcast(I32))
+            return words
+
         w1_raw = [load_rows(w1[a * PASS : (a + 1) * PASS, halves[0]]) for a in range(2)]
         idx = load_list(offs, "idx")
-        w2_raw = slot_tile([P, 2 * H], U8, "w2_raw", 6)
-        nc.sync.dma_start(w2_raw[:].bitcast(I32), w2_words[0].bitcast(I32))
         for quad in range(4):
             nc.sync.dma_start(
                 tab_planes[32 * quad : 32 * quad + 8, :].bitcast(I32),
                 tab_scales[:, 4 * quad : 4 * quad + 4, :].bitcast(I32),
             )
-        side_raw = load_rows(side[:, halves[0]])
+        tab = [load_tab(0)]
+        w2_raw = slot_tile([P, 2 * H], U8, "w2_raw", 6)
+        nc.sync.dma_start(w2_raw[:].bitcast(I32), w2_words[0].bitcast(I32))
+        side_raw = [load_rows(side[:, halves[0]])]
         for quad in range(4):
             nc.sync.dma_start(
                 w2_plane_raw[32 * quad : 32 * quad + 4, :].bitcast(I32),
                 w2_scales[0, 4 * quad : 4 * quad + 4, :].bitcast(I32),
             )
-        tab = []
-        for a in range(2):
-            words = big.tile([P, T], U32, name="tab%d" % a, offset=(4 + 2 * a) * PAGE_BYTES)
-            nc.sync.dma_start(words[:].bitcast(I32), tab_words[a].rearrange("p t i -> p (t i)").bitcast(I32))
-            tab.append(words)
+        w1_q = {(0, 0): quantize_rows_dealt(w1_raw[0], "w1_00", 0)}
+        side_raw.append(load_rows(side[:, halves[1]]))
+        tab.append(load_tab(1))
         gain_sb = keep.tile([P, H // PASS, PACK], F32, name="gain_sb")
         nc.sync.dma_start(gain_sb[:], gain.rearrange("(b p t) -> p b t", b=H // PASS, t=PACK))
-        idx2 = load_list(offs2, "idx2")
-        wg = {(0, 0): load_wgs(0, halves[0], "wg0_0")}
+        load_wgs(0, halves[0])
         pages = [load_page(0)]
+        idx2 = load_list(offs2, "idx2")
+        load_wgs(0, halves[1])
+        idx3 = load_list(offs3, "idx3")
+        idx4 = load_list(offs4, "idx4")
 
-        w1_q = {(0, 0): quantize_rows_dealt(w1_raw[0], "w1_00", 0)}
         picked_planes = keep.tile([P, S], U8, name="picked_planes", align_bytes=64)
         nc.vector.tensor_copy(picked_planes[:], tab_planes[:].indirect(idx[:]))
+        w1_q[1, 0] = quantize_rows_dealt(w1_raw[1], "w1_10", 1)
+
+        picked = [keep.tile([P, S], U32, name="picked%d" % a, align_bytes=64) for a in range(2)]
+
+        def list_columns(entries):
+            return slice(entries.start // 16, entries.stop // 16)
+
+        def pick_words(a, entries):
+            nc.vector.tensor_copy(picked[a][:, entries], tab[a][:].indirect(idx[:, list_columns(entries)]))
+
+        pick_words(0, slice(0, S))
         w2_codes = keep.tile([P, 2 * H], U8, name="w2_codes", align_bytes=64)
         nc.vector.tensor_copy(
             w2_codes[:].rearrange("p (b t m e) -> p b t m e", b=2, t=PACK, e=2),
             w2_raw[:].rearrange("p (b m t e) -> p b t m e", b=2, t=PACK, e=2),
         )
-        w1_q[1, 0] = quantize_rows_dealt(w1_raw[1], "w1_10", 1)
-        side_q = [quantize_rows(side_raw, "side0", 2)]
+        side_q = [quantize_rows(side_raw[0], "side0", 2)]
         w2_plane = keep.tile([P, H], U8, name="w2_plane", align_bytes=64)
         nc.vector.tensor_copy(
             w2_plane[:].rearrange("p (b t m) -> p b t m", b=2, t=PACK),
             w2_plane_raw[:].rearrange("p (b m t) -> p b t m", b=2, t=PACK),
         )
-
-        picked = {}
-
-        def pick_words(a, half):
-            tile = keep.tile([P, COLS], U32, name="picked%d_%d" % (a, half), align_bytes=64)
-            nc.vector.tensor_copy(tile[:], tab[a][:].indirect(idx[:, 32 * half : 32 * half + 32]))
-            picked[a, half] = tile
+        side_q.append(quantize_rows(side_raw[1], "side1", 3))
 
         h = {}
 
-        def first_stage(i, half):
+        def first_stage(i, entries):
             b, t = divmod(i, PACK)
-            bank = banks[half]
+            half, start = divmod(entries.start, COLS)
+            cols = slice(start, start + entries.stop - entries.start)
+            bank = banks[(half + start // QUARTER) % 2]
             nc.tensor.matmul_mx(
-                bank[:],
+                bank[:, cols],
                 lhsT=w2_codes[:, 2 * P * i : 2 * P * (i + 1)].bitcast(E2M1),
                 lhsT_scale=w2_plane[:, P * i : P * (i + 1)],
-                rhs=side_q[half][0][:].bitcast(E4M3),
-                rhs_scale=side_q[half][1][:],
+                rhs=side_q[half][0][:, cols].bitcast(E4M3),
+                rhs_scale=side_q[half][1][:, cols],
                 start=True,
                 stop=False,
             )
             for a in range(2):
                 codes, scales = w1_q[a, b]
                 nc.tensor.matmul_mx(
-                    bank[:],
+                    bank[:, cols],
                     lhsT=codes[:, P * t : P * (t + 1)].bitcast(E4M3),
                     lhsT_scale=scales[:, P * t : P * (t + 1)],
-                    rhs=picked[a, half][:].bitcast(E4M3),
-                    rhs_scale=picked_planes[4 * a :, halves[half]],
+                    rhs=picked[a][:, entries].bitcast(E4M3),
+                    rhs_scale=picked_planes[4 * a :, entries],
                     start=False,
                     stop=(a == 1),
                 )
-            tile = ring.tile([P, COLS], F32, name="h", tag="slab", bufs=16)
-            nc.scalar.activation(tile[:], bank[:], ACT.Gelu_apprx_tanh)
-            nc.scalar.activation(tile[:], tile[:], ACT.Copy, scale=gain_sb[:, b, t : t + 1])
-            h[i, half] = tile
+            if entries.start == 0:
+                h[i] = ring.tile([P, S], F32, name="h", tag="slab", bufs=ROW_TILES)
+            gelu = ring.tile([P, COLS], F32, name="gelu")
+            nc.scalar.activation(gelu[:, cols], bank[:, cols], ACT.Gelu_apprx_tanh)
+            nc.scalar.activation(h[i][:, entries], gelu[:, cols], ACT.Copy, scale=gain_sb[:, b, t : t + 1])
 
-        def put_h(i, half):
+        def put_h(i, entries):
             nc.vector.tensor_tensor(
-                pages[i][:].indirect(idx2[:, 32 * half : 32 * half + 32]),
-                h[i, half][:],
-                wg[i % PACK, half][:],
+                pages[i][:].indirect(idx2[:, list_columns(entries)]),
+                h[i][:, entries],
+                wg[i % PACK][:, entries],
                 ALU.mult,
             )
 
-        pick_words(0, 0)
-        pick_words(0, 1)
-        pick_words(1, 0)
-        first_stage(0, 0)
-        pick_words(1, 1)
-        put_h(0, 0)
-
-        side_raw = load_rows(side[:, halves[1]])
-        wg[0, 1] = load_wgs(0, halves[1], "wg0_1")
-        idx3 = load_list(offs3, "idx3")
-        idx4 = load_list(offs4, "idx4")
-        side_q.append(quantize_rows(side_raw, "side1", 3))
-        first_stage(0, 1)
-        put_h(0, 1)
+        for start in (0, QUARTER):
+            pick_words(1, slice(start, start + QUARTER))
+            first_stage(0, slice(start, start + QUARTER))
+        pick_words(1, halves[1])
+        put_h(0, slice(0, QUARTER))
+        put_h(0, slice(QUARTER, COLS))
+        first_stage(0, halves[1])
+        put_h(0, halves[1])
 
         def prepare(i):
             if i < PACK:
-                both = load_wgs(i, slice(0, S), "wg%d" % i)
-                wg[i, 0], wg[i, 1] = both[:, halves[0]], both[:, halves[1]]
+                load_wgs(i, slice(0, S))
             pages.append(load_page(i))
-            first_stage(i, 0)
-            first_stage(i, 1)
+            for entries in halves:
+                first_stage(i, entries)
 
         prepare(1)
         shift_sb = keep.tile([P, H // PASS, PACK], F32, name="shift_sb")
         nc.sync.dma_start(shift_sb[:], shift.rearrange("(b p t) -> p b t", b=H // PASS, t=PACK))
         for a in range(2):
-            w1_q[a, 1] = quantize_rows_dealt(load_rows(w1[a * PASS : (a + 1) * PASS, halves[1]]), "w1_%d1" % a, a)
-        prepare(2)
+            w1_q[a, 1] = quantize_rows_dealt(load_rows(w1[a * PASS : (a + 1) * PASS, halves[1]]), "w1_%d1" % a, 4 + a)
+        for i in range(2, 5):
+            prepare(i)
         w3_q = [quantize_rows(load_rows(w3[b * PASS : (b + 1) * PASS, :]), "w3_%d" % b, 6 + b) for b in range(2)]
-        for i in range(3, ROW_TILES):
+        for i in range(5, ROW_TILES):
             prepare(i)
 
         woven_page = {
@@ -231,8 +239,12 @@ def tile_list_stumpage_stand_appraisal_kernel(
         }
         page_q = {}
 
-        def quantize_page(b, c):
-            codes, scales = mx_tiles("page_%d%d" % (b, c))
+        def quantize_page(b, c, codes_slot=None):
+            if codes_slot is None:
+                codes, scales = mx_tiles("page_%d%d" % (b, c))
+            else:
+                codes = slot_tile([P, COLS], U32, "page_%d%d_codes" % (b, c), codes_slot)
+                scales = keep.tile([P, COLS], U8, name="page_%d%d_scales" % (b, c), align_bytes=64)
             nc.vector.quantize_mx(codes[:].bitcast(E4M3), scales[:], woven_page[b, c][:].rearrange("p c t -> p (c t)"))
             page_q[b, c] = codes, scales
 
@@ -250,31 +262,44 @@ def tile_list_stumpage_stand_appraisal_kernel(
                 stop=(b == 1),
             )
 
+        def fetch_first(i):
+            if i == 1:
+                tile = slot_tile([P, PAIRS], F32, "first1", 5)
+            elif i + 1 == ROW_TILES:
+                tile = slot_tile([P, PAIRS], F32, "first_last", 1)
+            else:
+                tile = ring.tile([P, PAIRS], F32, name="first")
+            nc.vector.tensor_copy(tile[:], pages[i][:].indirect(idx3[:]))
+            return tile
+
         marks_sb = []
+        first = fetch_first(0)
         for i in range(ROW_TILES):
             b, t = divmod(i, PACK)
             page = pages[i]
-            if i + 1 < ROW_TILES:
-                first = ring.tile([P, PAIRS], F32, name="first")
-            else:
-                first = slot_tile([P, PAIRS], F32, "first_last", CHUNKS - 1)
+            last = i + 1 == ROW_TILES
             second = ring.tile([P, PAIRS], F32, name="second")
-            lower = ring.tile([P, PAIRS], F32, name="lower")
-            nc.vector.tensor_copy(first[:], page[:].indirect(idx3[:]))
+            if last:
+                lower = slot_tile([P, PAIRS], F32, "lower_last", 0)
+            else:
+                lower = ring.tile([P, PAIRS], F32, name="lower")
             nc.vector.tensor_copy(second[:], page[:].indirect(idx4[:]))
-            if i + 1 < ROW_TILES:
-                put_h(i + 1, 0)
-            nc.vector.tensor_tensor(lower[:], first[:], second[:], ALU.min)
+            if not last:
+                put_h(i + 1, slice(0, S))
             nc.vector.tensor_tensor(page[:].indirect(idx4[:]), first[:], second[:], ALU.add)
-            if i + 1 < ROW_TILES:
-                put_h(i + 1, 1)
+            nc.vector.tensor_tensor(lower[:], first[:], second[:], ALU.min)
             if i == PACK:
-                for c in range(CHUNKS):
-                    quantize_page(0, c)
                 for c in range(BANKS // N_TILES):
+                    quantize_page(0, c)
                     for n in range(N_TILES):
                         second_stage(0, c, n)
+            if last:
+                quantize_page(0, 2, codes_slot=1)
+            else:
+                first = fetch_first(i + 1)
             nc.vector.tensor_copy(page[:].indirect(idx3[:]), lower[:])
+            if last:
+                quantize_page(0, 3, codes_slot=0)
             for c in range(CHUNKS):
                 nc.scalar.activation(
                     woven_page[b, c][:, :, t],
@@ -297,6 +322,6 @@ def tile_list_stumpage_stand_appraisal_kernel(
                 quantize_page(1, c + 1)
             for n in range(N_TILES):
                 cols = slice(c * COLS, (c + 1) * COLS)
-                result = ring.tile([P, COLS], F32, name="result", tag="slab", bufs=16)
+                result = ring.tile([P, COLS], F32, name="result", tag="slab", bufs=ROW_TILES)
                 nc.vector.tensor_tensor(result[:], bank_of(c, n)[:], marks_sb[n][:, cols], ALU.mult)
                 nc.sync.dma_start(out[P * n : P * (n + 1), cols], result[:])

@@ -49,18 +49,18 @@ def tile_list_stumpage_stand_appraisal_kernel(
             nc.sync.dma_start(tile[:], src)
             return tile
 
-        def mx_tiles(name):
-            codes = keep.tile([P, COLS], U32, name=name + "_codes", align_bytes=64)
-            scales = keep.tile([P, COLS], U8, name=name + "_scales", align_bytes=64)
+        def mx_tiles(name, width=COLS):
+            codes = keep.tile([P, width], U32, name=name + "_codes", align_bytes=64)
+            scales = keep.tile([P, width], U8, name=name + "_scales", align_bytes=64)
             return codes, scales
 
         def load_rows(rows):
-            raw = ring.tile([P, PACK, COLS], F32, name="raw", bufs=3)
+            raw = ring.tile([P, PACK, rows.shape[1]], F32, name="raw")
             nc.sync.dma_start(raw[:], rows.rearrange("(p j) c -> p j c", j=PACK))
             return raw
 
         def quantize(woven, name):
-            codes, scales = mx_tiles(name)
+            codes, scales = mx_tiles(name, woven.shape[1] // PACK)
             nc.vector.quantize_mx(codes[:].bitcast(E4M3), scales[:], woven[:])
             return codes, scales
 
@@ -68,7 +68,7 @@ def tile_list_stumpage_stand_appraisal_kernel(
             return slots.tile(shape, dtype, name=name, offset=slot * SLOT_BYTES, align_bytes=64)
 
         def quantize_rows(raw, name, slot):
-            woven = slot_tile([P, PACK * COLS], BF16, name + "_woven", slot)
+            woven = slot_tile([P, PACK * raw.shape[2]], BF16, name + "_woven", slot)
             nc.scalar.copy(
                 woven[:].rearrange("p (c i j) -> p c j i", i=4, j=PACK),
                 raw[:].rearrange("p j (c i) -> p c j i", i=4),
@@ -83,26 +83,18 @@ def tile_list_stumpage_stand_appraisal_kernel(
             )
             return quantize(woven, name)
 
-        page_rows = page0.rearrange("(b p t) c -> b t p c", b=H // PASS, t=PACK)
+        dealt_rows = page0[PASS:, :].rearrange("(p t) c -> t p c", t=PACK)
 
         def load_page(i):
             page = big.tile([P, T2], F32, name="page%d" % i, offset=i * PAGE_BYTES)
-            nc.sync.dma_start(page[:], page_rows[i // PACK, i % PACK])
+            nc.sync.dma_start(page[:], page0[P * i : P * (i + 1), :] if i < PACK else dealt_rows[i - PACK])
             return page
-
-        wgs_rows = wgs.rearrange("(q t) j -> t q j", t=PACK)
-
-        wg = [keep.tile([P, S], F32, name="wg%d" % t) for t in range(PACK)]
-
-        def load_wgs(t, cols):
-            for quad in range(4):
-                nc.sync.dma_start(wg[t][32 * quad : 32 * quad + 32, cols], wgs_rows[t][:, cols])
 
         halves = [slice(0, COLS), slice(COLS, 2 * COLS)]
 
         tab_planes = slot_tile([P, T], U8, "tab_planes", 4)
         nc.vector.memset(tab_planes[:].bitcast(I32), 0)
-        w2_plane_raw = slot_tile([P, H], U8, "w2_plane_raw", 5)
+        w2_plane_raw = keep.tile([P, H], U8, name="w2_plane_raw", align_bytes=64)
         nc.vector.memset(w2_plane_raw[:].bitcast(I32), 0)
 
         def load_tab(a):
@@ -110,37 +102,48 @@ def tile_list_stumpage_stand_appraisal_kernel(
             nc.sync.dma_start(words[:].bitcast(I32), tab_words[a].rearrange("p t i -> p (t i)").bitcast(I32))
             return words
 
-        w1_raw = [load_rows(w1[a * PASS : (a + 1) * PASS, halves[0]]) for a in range(2)]
+        def load_natural(vec, name):
+            tile = keep.tile([P, PACK], F32, name=name)
+            with nc.allow_non_contiguous_dma(reason="one value a partition"):
+                nc.sync.dma_start(tile[:], vec[:PASS].rearrange("(i p) -> p i", p=P))
+            return tile
+
+        def load_dealt(vec, name):
+            tile = keep.tile([P, PACK], F32, name=name)
+            nc.sync.dma_start(tile[:], vec[PASS:].rearrange("(p t) -> p t", t=PACK))
+            return tile
+
+        tab = [load_tab(0)]
+        side_raw = [load_rows(side[:, halves[0]])]
         idx = load_list(offs, "idx")
         for quad in range(4):
             nc.sync.dma_start(
                 tab_planes[32 * quad : 32 * quad + 8, :].bitcast(I32),
                 tab_scales[:, 4 * quad : 4 * quad + 4, :].bitcast(I32),
             )
-        tab = [load_tab(0)]
-        w2_raw = slot_tile([P, 2 * H], U8, "w2_raw", 6)
+        side_raw.append(load_rows(side[:, halves[1]]))
+        w1_first_raw = [slot_tile([P, PACK, P], F32, "w1_first_raw%d" % a, 6 + a) for a in range(2)]
+        for a in range(2):
+            nc.sync.dma_start(w1_first_raw[a][:], w1[a * PASS : (a + 1) * PASS, :P].rearrange("(p j) c -> p j c", j=PACK))
+        w2_raw = keep.tile([P, 2 * H], U8, name="w2_raw", align_bytes=64)
         nc.sync.dma_start(w2_raw[:].bitcast(I32), w2_words[0].bitcast(I32))
-        side_raw = [load_rows(side[:, halves[0]])]
+        tab.append(load_tab(1))
         for quad in range(4):
             nc.sync.dma_start(
                 w2_plane_raw[32 * quad : 32 * quad + 4, :].bitcast(I32),
                 w2_scales[0, 4 * quad : 4 * quad + 4, :].bitcast(I32),
             )
-        w1_q = {(0, 0): quantize_rows_dealt(w1_raw[0], "w1_00", 0)}
-        side_raw.append(load_rows(side[:, halves[1]]))
-        tab.append(load_tab(1))
-        gain_sb = keep.tile([P, H // PASS, PACK], F32, name="gain_sb")
-        nc.sync.dma_start(gain_sb[:], gain.rearrange("(b p t) -> p b t", b=H // PASS, t=PACK))
-        load_wgs(0, halves[0])
+        gain_sb = [load_natural(gain, "gain0")]
+        wg_natural = keep.tile([P, S], F32, name="wg_natural")
+        nc.sync.dma_start(wg_natural[:, halves[0]], wgs[:, halves[0]])
         pages = [load_page(0)]
         idx2 = load_list(offs2, "idx2")
-        load_wgs(0, halves[1])
+        nc.sync.dma_start(wg_natural[:, halves[1]], wgs[:, halves[1]])
         idx3 = load_list(offs3, "idx3")
         idx4 = load_list(offs4, "idx4")
 
         picked_planes = keep.tile([P, S], U8, name="picked_planes", align_bytes=64)
         nc.vector.tensor_copy(picked_planes[:], tab_planes[:].indirect(idx[:]))
-        w1_q[1, 0] = quantize_rows_dealt(w1_raw[1], "w1_10", 1)
 
         picked = [keep.tile([P, S], U32, name="picked%d" % a, align_bytes=64) for a in range(2)]
 
@@ -151,20 +154,22 @@ def tile_list_stumpage_stand_appraisal_kernel(
             nc.vector.tensor_copy(picked[a][:, entries], tab[a][:].indirect(idx[:, list_columns(entries)]))
 
         pick_words(0, slice(0, S))
-        w2_codes = keep.tile([P, 2 * H], U8, name="w2_codes", align_bytes=64)
+        side_q = [quantize_rows(side_raw[half], "side%d" % half, 2 + half) for half in range(2)]
+        w1_first = [quantize_rows(w1_first_raw[a], "w1_first%d" % a, a) for a in range(2)]
+        w2_codes = keep.tile([P, H], U8, name="w2_codes", align_bytes=64)
         nc.vector.tensor_copy(
-            w2_codes[:].rearrange("p (b t m e) -> p b t m e", b=2, t=PACK, e=2),
-            w2_raw[:].rearrange("p (b m t e) -> p b t m e", b=2, t=PACK, e=2),
+            w2_codes[:].rearrange("p (t m e) -> p t m e", t=PACK, e=2),
+            w2_raw[:, H:].rearrange("p (m t e) -> p t m e", t=PACK, e=2),
         )
-        side_q = [quantize_rows(side_raw[0], "side0", 2)]
-        w2_plane = keep.tile([P, H], U8, name="w2_plane", align_bytes=64)
-        nc.vector.tensor_copy(
-            w2_plane[:].rearrange("p (b t m) -> p b t m", b=2, t=PACK),
-            w2_plane_raw[:].rearrange("p (b m t) -> p b t m", b=2, t=PACK),
-        )
-        side_q.append(quantize_rows(side_raw[1], "side1", 3))
+
+        stationary = {}
+        for a in range(2):
+            stationary[a, 0] = w1_first[a][0][:], w1_first[a][1][:]
+        for i in range(PACK):
+            stationary[2, i] = w2_raw[:, 2 * P * i : 2 * P * (i + 1)], w2_plane_raw[:, P * i : P * (i + 1)]
 
         h = {}
+        wg = {i: wg_natural for i in range(PACK)}
 
         def first_stage(i, entries):
             b, t = divmod(i, PACK)
@@ -173,19 +178,19 @@ def tile_list_stumpage_stand_appraisal_kernel(
             bank = banks[(half + start // QUARTER) % 2]
             nc.tensor.matmul_mx(
                 bank[:, cols],
-                lhsT=w2_codes[:, 2 * P * i : 2 * P * (i + 1)].bitcast(E2M1),
-                lhsT_scale=w2_plane[:, P * i : P * (i + 1)],
+                lhsT=stationary[2, i][0].bitcast(E2M1),
+                lhsT_scale=stationary[2, i][1],
                 rhs=side_q[half][0][:, cols].bitcast(E4M3),
                 rhs_scale=side_q[half][1][:, cols],
                 start=True,
                 stop=False,
             )
             for a in range(2):
-                codes, scales = w1_q[a, b]
+                codes, scales = stationary[a, i]
                 nc.tensor.matmul_mx(
                     bank[:, cols],
-                    lhsT=codes[:, P * t : P * (t + 1)].bitcast(E4M3),
-                    lhsT_scale=scales[:, P * t : P * (t + 1)],
+                    lhsT=codes.bitcast(E4M3),
+                    lhsT_scale=scales,
                     rhs=picked[a][:, entries].bitcast(E4M3),
                     rhs_scale=picked_planes[4 * a :, entries],
                     start=False,
@@ -195,13 +200,13 @@ def tile_list_stumpage_stand_appraisal_kernel(
                 h[i] = ring.tile([P, S], F32, name="h", tag="slab", bufs=ROW_TILES)
             gelu = ring.tile([P, COLS], F32, name="gelu")
             nc.scalar.activation(gelu[:, cols], bank[:, cols], ACT.Gelu_apprx_tanh)
-            nc.scalar.activation(h[i][:, entries], gelu[:, cols], ACT.Copy, scale=gain_sb[:, b, t : t + 1])
+            nc.scalar.activation(h[i][:, entries], gelu[:, cols], ACT.Copy, scale=gain_sb[b][:, t : t + 1])
 
         def put_h(i, entries):
             nc.vector.tensor_tensor(
                 pages[i][:].indirect(idx2[:, list_columns(entries)]),
                 h[i][:, entries],
-                wg[i % PACK][:, entries],
+                wg[i][:, entries],
                 ALU.mult,
             )
 
@@ -215,23 +220,41 @@ def tile_list_stumpage_stand_appraisal_kernel(
         put_h(0, halves[1])
 
         def prepare(i):
-            if i < PACK:
-                load_wgs(i, slice(0, S))
             pages.append(load_page(i))
             for entries in halves:
                 first_stage(i, entries)
 
-        prepare(1)
-        shift_sb = keep.tile([P, H // PASS, PACK], F32, name="shift_sb")
-        nc.sync.dma_start(shift_sb[:], shift.rearrange("(b p t) -> p b t", b=H // PASS, t=PACK))
         for a in range(2):
-            w1_q[a, 1] = quantize_rows_dealt(load_rows(w1[a * PASS : (a + 1) * PASS, halves[1]]), "w1_%d1" % a, 4 + a)
-        for i in range(2, 5):
-            prepare(i)
-        w3_q = [quantize_rows(load_rows(w3[b * PASS : (b + 1) * PASS, :]), "w3_%d" % b, 6 + b) for b in range(2)]
+            codes, scales = quantize_rows(load_rows(w1[a * PASS : (a + 1) * PASS, P:PASS]), "w1_rest%d" % a, a)
+            for i in range(1, PACK):
+                stationary[a, i] = codes[:, P * (i - 1) : P * i], scales[:, P * (i - 1) : P * i]
+        prepare(1)
+        shift_sb = [load_natural(shift, "shift0"), load_dealt(shift, "shift1")]
+        gain_sb.append(load_dealt(gain, "gain1"))
+        w2_plane = keep.tile([P, PASS], U8, name="w2_plane", align_bytes=64)
+        nc.vector.tensor_copy(
+            w2_plane[:].rearrange("p (t m) -> p t m", t=PACK),
+            w2_plane_raw[:, PASS:].rearrange("p (m t) -> p t m", t=PACK),
+        )
+        for t in range(PACK):
+            stationary[2, PACK + t] = w2_codes[:, 2 * P * t : 2 * P * (t + 1)], w2_plane[:, P * t : P * (t + 1)]
+        for a in range(2):
+            codes, scales = quantize_rows_dealt(load_rows(w1[a * PASS : (a + 1) * PASS, PASS:]), "w1_dealt%d" % a, 2 + a)
+            for t in range(PACK):
+                stationary[a, PACK + t] = codes[:, P * t : P * (t + 1)], scales[:, P * t : P * (t + 1)]
+        prepare(2)
+        prepare(3)
+        wg_dealt = keep.tile([P, PACK, S], F32, name="wg_dealt")
+        for quad in range(4):
+            nc.sync.dma_start(wg_dealt[32 * quad : 32 * quad + 32], wgs.rearrange("(q t) j -> q t j", t=PACK))
+        for t in range(PACK):
+            wg[PACK + t] = wg_dealt[:, t, :]
+        prepare(4)
+        w3_q = [quantize_rows(load_rows(w3[b * PASS : (b + 1) * PASS, :]), "w3_%d" % b, b) for b in range(2)]
         for i in range(5, ROW_TILES):
             prepare(i)
 
+        planes = slot_tile([P, PACK, T2], BF16, "planes", 4)
         woven_page = {
             (b, c): slot_tile([P, COLS, PACK], BF16, "woven_page%d%d" % (b, c), CHUNKS * b + c)
             for b in range(H // PASS)
@@ -263,8 +286,8 @@ def tile_list_stumpage_stand_appraisal_kernel(
             )
 
         def fetch_first(i):
-            if i == 1:
-                tile = slot_tile([P, PAIRS], F32, "first1", 5)
+            if i < 2:
+                tile = slot_tile([P, PAIRS], F32, "first%d" % i, 1 + 2 * i)
             elif i + 1 == ROW_TILES:
                 tile = slot_tile([P, PAIRS], F32, "first_last", 1)
             else:
@@ -300,13 +323,25 @@ def tile_list_stumpage_stand_appraisal_kernel(
             nc.vector.tensor_copy(page[:].indirect(idx3[:]), lower[:])
             if last:
                 quantize_page(0, 3, codes_slot=0)
-            for c in range(CHUNKS):
-                nc.scalar.activation(
-                    woven_page[b, c][:, :, t],
-                    page[:, c * COLS : (c + 1) * COLS],
-                    ACT.Identity,
-                    bias=shift_sb[:, b, t : t + 1],
-                )
+            if b == 0:
+                rounded = keep.tile([P, T2], BF16, name="rounded")
+                nc.scalar.activation(rounded[:], page[:], ACT.Identity, bias=shift_sb[b][:, t : t + 1])
+                for j in range(PACK):
+                    nc.scalar.dma_start(planes[32 * i : 32 * i + 32, j, :], rounded[j:P:PACK, :])
+            else:
+                for c in range(CHUNKS):
+                    nc.scalar.activation(
+                        woven_page[b, c][:, :, t],
+                        page[:, c * COLS : (c + 1) * COLS],
+                        ACT.Identity,
+                        bias=shift_sb[b][:, t : t + 1],
+                    )
+            if i + 1 == PACK:
+                for c in range(CHUNKS):
+                    nc.scalar.copy(
+                        woven_page[0, c][:].rearrange("p (c i) j -> p c j i", i=4),
+                        planes[:, :, c * COLS : (c + 1) * COLS].rearrange("p j (c i) -> p c j i", i=4),
+                    )
             if i < N_TILES:
                 tile = big.tile([P, T2], F32, name="marks%d" % i, offset=i * PAGE_BYTES)
                 nc.sync.dma_start(tile[:], marks[P * i : P * (i + 1), :])

@@ -113,11 +113,11 @@ def tile_list_stumpage_stand_appraisal_kernel(
             nc.sync.dma_start(tile[:], vec[PASS:].rearrange("(p t) -> p t", t=PACK))
             return tile
 
+        idx = load_list(offs, "idx")
         tab = [load_tab(0)]
         side_raw = [load_rows(side[:, halves[0]])]
-        idx = load_list(offs, "idx")
         for quad in range(4):
-            nc.sync.dma_start(
+            nc.gpsimd.dma_start(
                 tab_planes[32 * quad : 32 * quad + 8, :].bitcast(I32),
                 tab_scales[:, 4 * quad : 4 * quad + 4, :].bitcast(I32),
             )
@@ -129,7 +129,7 @@ def tile_list_stumpage_stand_appraisal_kernel(
         nc.sync.dma_start(w2_raw[:].bitcast(I32), w2_words[0].bitcast(I32))
         tab.append(load_tab(1))
         for quad in range(4):
-            nc.sync.dma_start(
+            nc.gpsimd.dma_start(
                 w2_plane_raw[32 * quad : 32 * quad + 4, :].bitcast(I32),
                 w2_scales[0, 4 * quad : 4 * quad + 4, :].bitcast(I32),
             )

from contextlib import ExitStack

import concourse.mybir as mybir

K, K2, H, N, T, S, T2, PAIRS = 1024, 512, 1024, 512, 4096, 1024, 2048, 512
FLOPS = 2 * (K * H * S + K2 * H * S + H * N * T2)

F32 = mybir.dt.float32
BF16 = mybir.dt.bfloat16
I32 = mybir.dt.int32
U32 = mybir.dt.uint32
U16 = mybir.dt.uint16
U8 = mybir.dt.uint8
E4M3 = mybir.dt.float8_e4m3fn_x4
E2M1 = mybir.dt.float4_e2m1fn_x4
ACT = mybir.ActivationFunctionType
ALU = mybir.AluOpType

P = 128
PACK = 4
PASS = P * PACK
COLS = 512
QUARTER = 256
ROW_TILES = H // P
CHUNKS = T2 // COLS
N_TILES = N // P
BANKS = 8
PAGE_BYTES = T2 * 4
SLOT_BYTES = PACK * COLS * 2


def tile_list_stumpage_stand_appraisal_kernel(
    tc, tab_words, tab_scales, offs, offs2, offs3, offs4, w1, side, w2_words, w2_scales,
    gain, wgs, page0, shift, w3, marks, out,
):
    nc = tc.nc
    with ExitStack() as ctx:
        lists = ctx.enter_context(tc.tile_pool(name="lists", bufs=1))
        keep = ctx.enter_context(tc.tile_pool(name="keep", bufs=1))
        big = ctx.enter_context(tc.tile_pool(name="big", bufs=1))
        slots = ctx.enter_context(tc.tile_pool(name="slots", bufs=1))
        ring = ctx.enter_context(tc.tile_pool(name="ring", bufs=2))
        psum = ctx.enter_context(tc.psum_pool(name="psum", bufs=1))

        banks = [psum.tile([P, COLS], F32, name="bank%d" % b) for b in range(BANKS)]

        def load_list(src, name):
            tile = lists.tile(list(src.shape), U16, name=name)
            nc.sync.dma_start(tile[:], src)
            return tile

        def mx_tiles(name, width=COLS):
            codes = keep.tile([P, width], U32, name=name + "_codes", align_bytes=64)
            scales = keep.tile([P, width], U8, name=name + "_scales", align_bytes=64)
            return codes, scales

        def load_rows(rows):
            raw = ring.tile([P, PACK, rows.shape[1]], F32, name="raw")
            nc.sync.dma_start(raw[:], rows.rearrange("(p j) c -> p j c", j=PACK))
            return raw

        def quantize(woven, name):
            codes, scales = mx_tiles(name, woven.shape[1] // PACK)
            nc.vector.quantize_mx(codes[:].bitcast(E4M3), scales[:], woven[:])
            return codes, scales

        def slot_tile(shape, dtype, name, slot):
            return slots.tile(shape, dtype, name=name, offset=slot * SLOT_BYTES, align_bytes=64)

        def quantize_rows(raw, name, slot):
            woven = slot_tile([P, PACK * raw.shape[2]], BF16, name + "_woven", slot)
            nc.scalar.copy(
                woven[:].rearrange("p (c i j) -> p c j i", i=4, j=PACK),
                raw[:].rearrange("p j (c i) -> p c j i", i=4),
            )
            return quantize(woven, name)

        def quantize_rows_dealt(raw, name, slot):
            woven = slot_tile([P, PACK * COLS], BF16, name + "_woven", slot)
            nc.scalar.copy(
                woven[:].rearrange("p (t m j) -> p m t j", t=PACK, j=PACK),
                raw[:].rearrange("p j (m t) -> p m t j", t=PACK),
            )
            return quantize(woven, name)

        dealt_rows = page0[PASS:, :].rearrange("(p t) c -> t p c", t=PACK)

        def load_page(i):
            page = big.tile([P, T2], F32, name="page%d" % i, offset=i * PAGE_BYTES)
            nc.sync.dma_start(page[:], page0[P * i : P * (i + 1), :] if i < PACK else dealt_rows[i - PACK])
            return page

        halves = [slice(0, COLS), slice(COLS, 2 * COLS)]

        tab_planes = slot_tile([P, T], U8, "tab_planes", 4)
        nc.vector.memset(tab_planes[:].bitcast(I32), 0)
        w2_plane_raw = keep.tile([P, H], U8, name="w2_plane_raw", align_bytes=64)
        nc.vector.memset(w2_plane_raw[:].bitcast(I32), 0)

        def load_tab(a):
            words = big.tile([P, T], U32, name="tab%d" % a, offset=(4 + 2 * a) * PAGE_BYTES)
            nc.sync.dma_start(words[:].bitcast(I32), tab_words[a].rearrange("p t i -> p (t i)").bitcast(I32))
            return words

        def load_natural(vec, name):
            tile = keep.tile([P, PACK], F32, name=name)
            with nc.allow_non_contiguous_dma(reason="one value a partition"):
                nc.sync.dma_start(tile[:], vec[:PASS].rearrange("(i p) -> p i", p=P))
            return tile

        def load_dealt(vec, name):
            tile = keep.tile([P, PACK], F32, name=name)
            nc.sync.dma_start(tile[:], vec[PASS:].rearrange("(p t) -> p t", t=PACK))
            return tile

        idx = load_list(offs, "idx")
        tab = [load_tab(0)]
        side_raw = [load_rows(side[:, halves[0]])]
        for quad in range(4):
            nc.gpsimd.dma_start(
                tab_planes[32 * quad : 32 * quad + 8, :].bitcast(I32),
                tab_scales[:, 4 * quad : 4 * quad + 4, :].bitcast(I32),
            )
        side_raw.append(load_rows(side[:, halves[1]]))
        w1_first_raw = [slot_tile([P, PACK, P], F32, "w1_first_raw%d" % a, 6 + a) for a in range(2)]
        for a in range(2):
            nc.sync.dma_start(w1_first_raw[a][:], w1[a * PASS : (a + 1) * PASS, :P].rearrange("(p j) c -> p j c", j=PACK))
        w2_raw = keep.tile([P, 2 * H], U8, name="w2_raw", align_bytes=64)
        nc.sync.dma_start(w2_raw[:].bitcast(I32), w2_words[0].bitcast(I32))
        tab.append(load_tab(1))
        for quad in range(4):
            nc.gpsimd.dma_start(
                w2_plane_raw[32 * quad : 32 * quad + 4, :].bitcast(I32),
                w2_scales[0, 4 * quad : 4 * quad + 4, :].bitcast(I32),
            )
        gain_sb = [load_natural(gain, "gain0")]
        wg_natural = keep.tile([P, S], F32, name="wg_natural")
        nc.sync.dma_start(wg_natural[:, halves[0]], wgs[:, halves[0]])
        pages = [load_page(0)]
        idx2 = load_list(offs2, "idx2")
        nc.sync.dma_start(wg_natural[:, halves[1]], wgs[:, halves[1]])
        idx3 = load_list(offs3, "idx3")
        idx4 = load_list(offs4, "idx4")

        picked_planes = keep.tile([P, S], U8, name="picked_planes", align_bytes=64)
        nc.vector.tensor_copy(picked_planes[:], tab_planes[:].indirect(idx[:]))

        picked = [keep.tile([P, S], U32, name="picked%d" % a, align_bytes=64) for a in range(2)]

        def list_columns(entries):
            return slice(entries.start // 16, entries.stop // 16)

        def pick_words(a, entries):
            nc.vector.tensor_copy(picked[a][:, entries], tab[a][:].indirect(idx[:, list_columns(entries)]))

        pick_words(0, slice(0, S))
        side_q = [quantize_rows(side_raw[half], "side%d" % half, 2 + half) for half in range(2)]
        w1_first = [quantize_rows(w1_first_raw[a], "w1_first%d" % a, a) for a in range(2)]
        w2_codes = keep.tile([P, H], U8, name="w2_codes", align_bytes=64)
        nc.vector.tensor_copy(
            w2_codes[:].rearrange("p (t m e) -> p t m e", t=PACK, e=2),
            w2_raw[:, H:].rearrange("p (m t e) -> p t m e", t=PACK, e=2),
        )

        stationary = {}
        for a in range(2):
            stationary[a, 0] = w1_first[a][0][:], w1_first[a][1][:]
        for i in range(PACK):
            stationary[2, i] = w2_raw[:, 2 * P * i : 2 * P * (i + 1)], w2_plane_raw[:, P * i : P * (i + 1)]

        h = {}
        wg = {i: wg_natural for i in range(PACK)}

        def first_stage(i, entries):
            b, t = divmod(i, PACK)
            half, start = divmod(entries.start, COLS)
            cols = slice(start, start + entries.stop - entries.start)
            bank = banks[(half + start // QUARTER) % 2]
            nc.tensor.matmul_mx(
                bank[:, cols],
                lhsT=stationary[2, i][0].bitcast(E2M1),
                lhsT_scale=stationary[2, i][1],
                rhs=side_q[half][0][:, cols].bitcast(E4M3),
                rhs_scale=side_q[half][1][:, cols],
                start=True,
                stop=False,
            )
            for a in range(2):
                codes, scales = stationary[a, i]
                nc.tensor.matmul_mx(
                    bank[:, cols],
                    lhsT=codes.bitcast(E4M3),
                    lhsT_scale=scales,
                    rhs=picked[a][:, entries].bitcast(E4M3),
                    rhs_scale=picked_planes[4 * a :, entries],
                    start=False,
                    stop=(a == 1),
                )
            if entries.start == 0:
                h[i] = ring.tile([P, S], F32, name="h", tag="slab", bufs=ROW_TILES)
            gelu = ring.tile([P, COLS], F32, name="gelu")
            nc.scalar.activation(gelu[:, cols], bank[:, cols], ACT.Gelu_apprx_tanh)
            nc.scalar.activation(h[i][:, entries], gelu[:, cols], ACT.Copy, scale=gain_sb[b][:, t : t + 1])

        def put_h(i, entries):
            nc.vector.tensor_tensor(
                pages[i][:].indirect(idx2[:, list_columns(entries)]),
                h[i][:, entries],
                wg[i][:, entries],
                ALU.mult,
            )

        for start in (0, QUARTER):
            pick_words(1, slice(start, start + QUARTER))
            first_stage(0, slice(start, start + QUARTER))
        pick_words(1, halves[1])
        put_h(0, slice(0, QUARTER))
        put_h(0, slice(QUARTER, COLS))
        first_stage(0, halves[1])
        put_h(0, halves[1])

        def prepare(i):
            pages.append(load_page(i))
            for entries in halves:
                first_stage(i, entries)

        for a in range(2):
            codes, scales = quantize_rows(load_rows(w1[a * PASS : (a + 1) * PASS, P:PASS]), "w1_rest%d" % a, a)
            for i in range(1, PACK):
                stationary[a, i] = codes[:, P * (i - 1) : P * i], scales[:, P * (i - 1) : P * i]
        prepare(1)
        shift_sb = [load_natural(shift, "shift0"), load_dealt(shift, "shift1")]
        gain_sb.append(load_dealt(gain, "gain1"))
        w2_plane = keep.tile([P, PASS], U8, name="w2_plane", align_bytes=64)
        nc.vector.tensor_copy(
            w2_plane[:].rearrange("p (t m) -> p t m", t=PACK),
            w2_plane_raw[:, PASS:].rearrange("p (m t) -> p t m", t=PACK),
        )
        for t in range(PACK):
            stationary[2, PACK + t] = w2_codes[:, 2 * P * t : 2 * P * (t + 1)], w2_plane[:, P * t : P * (t + 1)]
        for a in range(2):
            codes, scales = quantize_rows_dealt(load_rows(w1[a * PASS : (a + 1) * PASS, PASS:]), "w1_dealt%d" % a, 2 + a)
            for t in range(PACK):
                stationary[a, PACK + t] = codes[:, P * t : P * (t + 1)], scales[:, P * t : P * (t + 1)]
        prepare(2)
        prepare(3)
        wg_dealt = keep.tile([P, PACK, S], F32, name="wg_dealt")
        for quad in range(4):
            nc.sync.dma_start(wg_dealt[32 * quad : 32 * quad + 32], wgs.rearrange("(q t) j -> q t j", t=PACK))
        for t in range(PACK):
            wg[PACK + t] = wg_dealt[:, t, :]
        prepare(4)
        w3_q = [quantize_rows(load_rows(w3[b * PASS : (b + 1) * PASS, :]), "w3_%d" % b, b) for b in range(2)]
        for i in range(5, ROW_TILES):
            prepare(i)

        planes = slot_tile([P, PACK, T2], BF16, "planes", 4)
        woven_page = {
            (b, c): slot_tile([P, COLS, PACK], BF16, "woven_page%d%d" % (b, c), CHUNKS * b + c)
            for b in range(H // PASS)
            for c in range(CHUNKS)
        }
        page_q = {}

        def quantize_page(b, c, codes_slot=None):
            if codes_slot is None:
                codes, scales = mx_tiles("page_%d%d" % (b, c))
            else:
                codes = slot_tile([P, COLS], U32, "page_%d%d_codes" % (b, c), codes_slot)
                scales = keep.tile([P, COLS], U8, name="page_%d%d_scales" % (b, c), align_bytes=64)
            nc.vector.quantize_mx(codes[:].bitcast(E4M3), scales[:], woven_page[b, c][:].rearrange("p c t -> p (c t)"))
            page_q[b, c] = codes, scales

        def bank_of(c, n):
            return banks[(c * N_TILES + n + 2) % BANKS]

        def second_stage(b, c, n):
            nc.tensor.matmul_mx(
                bank_of(c, n)[:],
                lhsT=w3_q[b][0][:, P * n : P * (n + 1)].bitcast(E4M3),
                lhsT_scale=w3_q[b][1][:, P * n : P * (n + 1)],
                rhs=page_q[b, c][0][:].bitcast(E4M3),
                rhs_scale=page_q[b, c][1][:],
                start=(b == 0),
                stop=(b == 1),
            )

        def fetch_first(i):
            if i < 2:
                tile = slot_tile([P, PAIRS], F32, "first%d" % i, 1 + 2 * i)
            elif i + 1 == ROW_TILES:
                tile = slot_tile([P, PAIRS], F32, "first_last", 1)
            else:
                tile = ring.tile([P, PAIRS], F32, name="first")
            nc.vector.tensor_copy(tile[:], pages[i][:].indirect(idx3[:]))
            return tile

        marks_sb = []
        first = fetch_first(0)
        for i in range(ROW_TILES):
            b, t = divmod(i, PACK)
            page = pages[i]
            last = i + 1 == ROW_TILES
            second = ring.tile([P, PAIRS], F32, name="second")
            if last:
                lower = slot_tile([P, PAIRS], F32, "lower_last", 0)
            else:
                lower = ring.tile([P, PAIRS], F32, name="lower")
            nc.vector.tensor_copy(second[:], page[:].indirect(idx4[:]))
            if not last:
                put_h(i + 1, slice(0, S))
            nc.vector.tensor_tensor(page[:].indirect(idx4[:]), first[:], second[:], ALU.add)
            nc.vector.tensor_tensor(lower[:], first[:], second[:], ALU.min)
            if i == PACK:
                for c in range(BANKS // N_TILES):
                    quantize_page(0, c)
                    for n in range(N_TILES):
                        second_stage(0, c, n)
            if last:
                quantize_page(0, 2, codes_slot=1)
            else:
                first = fetch_first(i + 1)
            nc.vector.tensor_copy(page[:].indirect(idx3[:]), lower[:])
            if last:
                quantize_page(0, 3, codes_slot=0)
            if b == 0:
                rounded = keep.tile([P, T2], BF16, name="rounded")
                nc.scalar.activation(rounded[:], page[:], ACT.Identity, bias=shift_sb[b][:, t : t + 1])
                for j in range(PACK):
                    nc.scalar.dma_start(planes[32 * i : 32 * i + 32, j, :], rounded[j:P:PACK, :])
            else:
                for c in range(CHUNKS):
                    nc.scalar.activation(
                        woven_page[b, c][:, :, t],
                        page[:, c * COLS : (c + 1) * COLS],
                        ACT.Identity,
                        bias=shift_sb[b][:, t : t + 1],
                    )
            if i + 1 == PACK:
                for c in range(CHUNKS):
                    nc.scalar.copy(
                        woven_page[0, c][:].rearrange("p (c i) j -> p c j i", i=4),
                        planes[:, :, c * COLS : (c + 1) * COLS].rearrange("p j (c i) -> p c j i", i=4),
                    )
            if i < N_TILES:
                tile = big.tile([P, T2], F32, name="marks%d" % i, offset=i * PAGE_BYTES)
                nc.sync.dma_start(tile[:], marks[P * i : P * (i + 1), :])
                marks_sb.append(tile)

        quantize_page(1, 0)
        for c in range(CHUNKS):
            for n in range(N_TILES):
                if c >= BANKS // N_TILES:
                    second_stage(0, c, n)
                second_stage(1, c, n)
            if c + 1 < CHUNKS:
                quantize_page(1, c + 1)
            for n in range(N_TILES):
                cols = slice(c * COLS, (c + 1) * COLS)
                result = ring.tile([P, COLS], F32, name="result", tag="slab", bufs=ROW_TILES)
                nc.vector.tensor_tensor(result[:], bank_of(c, n)[:], marks_sb[n][:, cols], ALU.mult)
                nc.sync.dma_start(out[P * n : P * (n + 1), cols], result[:])
